import numpy as np
import ml_dtypes


def mxq(x, axis, fmt="e4m3"):
    dtype, down = {"e4m3": (ml_dtypes.float8_e4m3fn, 7), "e5m2": (ml_dtypes.float8_e5m2, 14)}[fmt]
    v = np.moveaxis(np.asarray(x, np.float32).astype(ml_dtypes.bfloat16).astype(np.float64), axis, -1)
    blocks = v.reshape(v.shape[:-1] + (-1, 32))
    amax = np.abs(blocks).max(-1, keepdims=True)
    byte = np.maximum(np.where(amax > 0, np.frexp(amax)[1] - 1 + 127, 0) - down, 1)
    scale = np.exp2(byte - 127.0)
    codes = (blocks / scale).astype(np.float32).astype(dtype).astype(np.float64)
    return np.moveaxis((codes * scale).reshape(v.shape), -1, axis)


WIDE = False


def mx_kscale(k):
    if not WIDE:
        return np.ones(k)
    levels = np.array([10, -10, 5, -5, 0])
    if k % 512:
        return np.exp2(np.random.permutation(np.resize(levels, k // 32))).repeat(32)
    a = np.empty((k // 512, 16))
    for p in range(k // 512):
        a[p, :8] = np.random.permutation(np.resize(levels, 8))
        for g in range(8):
            far = levels[np.abs(levels - a[p, g]) >= 10]
            a[p, g + 8] = far[np.random.randint(len(far))]
    return np.exp2(a.ravel()).repeat(32)


def f64(x):
    return np.asarray(x).astype(np.float64)


def striped(idx):
    return np.tile(idx.reshape(-1, 16).T, (8, 1)).astype(np.uint16)


def unstriped(offs):
    return offs[:16].T.reshape(-1).astype(np.int64)


E2M1 = np.array([0.0, 0.5, 1.0, 1.5, 2.0, 3.0, 4.0, 6.0, -0.0, -0.5, -1.0, -1.5, -2.0, -3.0, -4.0, -6.0])


def pack_weight(w, fmt):
    k, n = w.shape
    w = f64(np.asarray(w, np.float32).astype(ml_dtypes.bfloat16)).reshape(k // 32, 32, n)
    amax = np.abs(w).max(1)
    if fmt == "e4m3":
        byte = np.frexp(amax)[1] - 1 + 127 - 7
    else:
        mant, ex = np.frexp(amax / 6.0)
        byte = np.where(mant > 0.5, ex, ex - 1) + 127
    byte = np.clip(np.where(amax > 0, byte, 1), 1, 254)
    scaled = (w * np.exp2(127.0 - byte)[:, None, :]).reshape(k, n).astype(np.float32)
    by_word = np.ascontiguousarray(scaled.reshape(k // 512, 128, 4, n).transpose(0, 1, 3, 2))
    if fmt == "e4m3":
        words = by_word.astype(ml_dtypes.float8_e4m3fn).view(np.uint8)
    else:
        c = by_word.astype(ml_dtypes.float4_e2m1fn).view(np.uint8) & 0xF
        words = (c[..., 0::2] | (c[..., 1::2] << 4)).reshape(k // 512, 128, 2 * n)
    return np.ascontiguousarray(words), np.ascontiguousarray(byte.astype(np.uint8).reshape(k // 512, 16, n))


def unpack_weight(words, scales, fmt):
    g, _, n = scales.shape
    words = np.ascontiguousarray(words).reshape(g, 128, n, -1)
    if fmt == "e4m3":
        vals = words.view(ml_dtypes.float8_e4m3fn).astype(np.float64)
    else:
        nib = np.empty((g, 128, n, 4), np.uint8)
        nib[..., 0::2] = words & 0xF
        nib[..., 1::2] = words >> 4
        vals = E2M1[nib]
    vals = vals * np.repeat(np.exp2(scales.astype(np.float64) - 127.0), 8, axis=1)[..., None]
    return vals.transpose(0, 1, 3, 2).reshape(g * 512, n)


def gelu(v):
    return 0.5 * v * (1.0 + np.tanh(np.sqrt(2.0 / np.pi) * (v + 0.044715 * v**3)))


K, H, T, S, T2, P = 1536, 512, 4096, 1024, 2048, 1024

def setup_inputs():
    n = np.random.standard_normal
    s = mx_kscale(K)[:, None]
    u = mx_kscale(H)[:, None]
    d = {}
    d["tab_words"], d["tab_scales"] = pack_weight(n((K, T)) * s, "e4m3")
    d["offs"] = striped(np.random.permutation(T)[:S])
    d["offs2"] = striped(np.random.permutation(T2)[:S])
    d["offs3"] = striped(np.random.permutation(T2)[:P])
    d["offs4"] = striped(np.random.permutation(T2)[:P])
    d["w1"] = (n((K, H)) / K ** 0.5 / s * u.T).astype(np.float32)
    d["w4_words"], d["w4_scales"] = pack_weight(n((H, H)) / H ** 0.5 / u, "e2m1")
    d["w8_words"], d["w8_scales"] = pack_weight(1.6 * n((H, H)) / H ** 0.5 / u, "e4m3")
    d["wgs"] = np.exp(0.3 * n((128, S))).astype(np.float32)
    d["page0"] = (n((H, T2)) * u).astype(np.float32)
    d["sc"] = (1.3 * np.exp(0.2 * n(H)) / u[:, 0]).astype(np.float32)
    d["amp"] = (np.exp(0.3 * n(H)) * u[:, 0]).astype(np.float32)
    d["beta"] = (np.exp(0.3 * n(H)) / u[:, 0]).astype(np.float32)
    return d

def reference(tab_words, tab_scales, offs, offs2, offs3, offs4, w1, w4_words, w4_scales,
              w8_words, w8_scales, wgs, page0, sc, amp, beta):
    v = unpack_weight(tab_words, tab_scales, "e4m3")[:, unstriped(offs)]
    a = mxq(f64(w1), 0, "e4m3").T @ v
    b = unpack_weight(w4_words, w4_scales, "e2m1").T @ mxq(a, 0, "e4m3")
    h = a * b
    page = f64(page0).copy()
    page[:, unstriped(offs2)] = np.tile(f64(wgs), (H // 128, 1)) * h
    x = f64(amp)[:, None] * np.tanh(f64(sc)[:, None] * page[:, unstriped(offs3)])
    y = unpack_weight(w8_words, w8_scales, "e4m3").T @ mxq(x, 0, "e4m3")
    return f64(beta)[:, None] * page[:, unstriped(offs4)] - np.abs(y)

@@ -1,0 +1,327 @@
+from contextlib import ExitStack
+
+import concourse.mybir as mybir
+
+K, H, T, S, T2, M = 1536, 512, 4096, 1024, 2048, 1024
+FLOPS = 2 * K * H * S + 2 * H * H * S + 2 * H * H * M
+
+F32 = mybir.dt.float32
+BF16 = mybir.dt.bfloat16
+I32 = mybir.dt.int32
+U32 = mybir.dt.uint32
+U16 = mybir.dt.uint16
+U8 = mybir.dt.uint8
+FP8X4 = mybir.dt.float8_e4m3fn_x4
+FP4X4 = mybir.dt.float4_e2m1fn_x4
+ALU = mybir.AluOpType
+ACT = mybir.ActivationFunctionType
+
+P = 128
+PACK = 4
+PASSES = K // (P * PACK)
+CHUNK = 128
+HALF = 512
+RUN = 256
+
+
+def tile_list_marble_bench_register_kernel(
+    tc, tab_words, tab_scales, offs, offs2, offs3, offs4, w1, w4_words, w4_scales,
+    w8_words, w8_scales, wgs, page0, sc, amp, beta, out,
+):
+    nc = tc.nc
+    with ExitStack() as ctx:
+        lists = ctx.enter_context(tc.tile_pool(name="lists", bufs=1))
+        keep = ctx.enter_context(tc.tile_pool(name="keep", bufs=1))
+        psum = ctx.enter_context(tc.psum_pool(name="psum", bufs=1))
+
+        def tile(shape, dtype, name, tag=None):
+            return keep.tile(shape, dtype, name=name, tag=tag or name, align_bytes=64)
+
+        def bank(shape, name, number):
+            return psum.tile(shape, F32, name=name, tag="bank%d" % number)
+
+        def load_list(source, name):
+            held = lists.tile([P, S // 16], U16, name=name)
+            nc.sync.dma_start(held[:], source)
+            return held
+
+        def entries(held, first, count):
+            return held[:, first // 16 : (first + count) // 16]
+
+        table_scales = tile([P, T], U8, "table_scales")
+        nc.vector.memset(table_scales[:].bitcast(I32), 0)
+        weight_scales = tile([P, 2, H], U8, "weight_scales")
+        nc.vector.memset(weight_scales[:].rearrange("p i c -> p (i c)").bitcast(I32), 0)
+        for q in range(4):
+            nc.gpsimd.dma_start(
+                out=table_scales[32 * q : 32 * q + 4 * PASSES, :].bitcast(I32),
+                in_=tab_scales[:, 4 * q : 4 * q + 4, :].bitcast(I32),
+            )
+
+        def load_weight_scales(i, source):
+            for q in range(4):
+                nc.sync.dma_start(
+                    out=weight_scales[32 * q : 32 * q + 4, i, :].bitcast(I32),
+                    in_=source[0, 4 * q : 4 * q + 4, :].bitcast(I32),
+                )
+
+        def load_factor(source, name):
+            factor = tile([P, PACK], F32, name)
+            nc.sync.dma_start(out=factor[:], in_=source.rearrange("(p t) -> p t", t=PACK))
+            return factor
+
+        table = [tile([P, T], U32, "table%d" % a) for a in range(PASSES)]
+        w1_raw = [tile([P, PACK, H], F32, "w1_raw%d" % a, "wide%d" % a) for a in range(PASSES)]
+
+        def load_table(a):
+            nc.sync.dma_start(
+                out=table[a][:].bitcast(I32),
+                in_=tab_words[a].rearrange("p t i -> p (t i)").bitcast(I32),
+            )
+
+        def load_w1(a):
+            nc.sync.dma_start(
+                out=w1_raw[a][:],
+                in_=w1[a * HALF : (a + 1) * HALF, :].rearrange("(p j) c -> p j c", j=PACK),
+            )
+
+        load_table(0)
+        idx = load_list(offs, "idx")
+        load_w1(0)
+        w4_raw = tile([P, 2 * H], U8, "w4_raw")
+        nc.sync.dma_start(out=w4_raw[:].bitcast(I32), in_=w4_words[0].bitcast(I32))
+        idx2 = load_list(offs2, "idx2")
+        idx3 = load_list(offs3, "idx3")
+        idx4 = load_list(offs4, "idx4")
+        sc_rows = load_factor(sc, "sc_rows")
+        load_w1(1)
+        load_w1(2)
+        load_weight_scales(0, w4_scales)
+        load_table(1)
+        load_table(2)
+        w8_raw = tile([P, H], I32, "w8_raw")
+        nc.sync.dma_start(out=w8_raw[:], in_=w8_words[0].rearrange("p c i -> p (c i)").bitcast(I32))
+        load_weight_scales(1, w8_scales)
+
+        page = [tile([P, T2], F32, "page%d" % t) for t in range(PACK)]
+        gain = tile([P, PACK, S], F32, "gain")
+        page_rows = page0.rearrange("(p t) c -> t p c", t=PACK)
+        gain_rows = wgs.rearrange("(p t) j -> p t j", t=PACK)
+
+        def load_gain(first, count):
+            for q in (0, 2, 1, 3):
+                nc.sync.dma_start(
+                    out=gain[32 * q : 32 * q + 32, :, first : first + count],
+                    in_=gain_rows[:, :, first : first + count],
+                )
+
+        nc.sync.dma_start(out=page[0][:], in_=page_rows[0])
+        load_gain(0, RUN)
+        nc.sync.dma_start(out=page[1][:], in_=page_rows[1])
+        load_gain(RUN, RUN)
+        nc.sync.dma_start(out=page[2][:], in_=page_rows[2])
+        nc.sync.dma_start(out=page[3][:], in_=page_rows[3])
+        load_gain(HALF, HALF)
+        amp_rows = load_factor(amp, "amp_rows")
+        beta_rows = load_factor(beta, "beta_rows")
+
+        w1_codes, w1_scales = [], []
+        for a in range(PASSES):
+            woven = tile([P, PACK, P, PACK], BF16, "w1_woven%d" % a, "narrow%d" % a)
+            nc.scalar.copy(
+                out=woven[:].rearrange("p t m j -> p m j t"),
+                in_=w1_raw[a][:].rearrange("p j (m t) -> p m j t", t=PACK),
+            )
+            codes = tile([P, H], U32, "w1_codes%d" % a)
+            scales = tile([P, H], U8, "w1_scales%d" % a)
+            nc.vector.quantize_mx(
+                out=codes[:].bitcast(FP8X4), scales=scales[:],
+                in_=woven[:].rearrange("p t m j -> p (t m j)"),
+            )
+            w1_codes.append(codes)
+            w1_scales.append(scales)
+
+        picked_scales = tile([P, S], U8, "picked_scales")
+        nc.vector.tensor_copy(picked_scales[:], table_scales[:].indirect(idx[:]))
+
+        dealt_scales = tile([P, 2, PACK, P], U8, "dealt_scales")
+
+        def deal_scales(i):
+            nc.vector.tensor_copy(
+                out=dealt_scales[:, i, :, :], in_=weight_scales[:, i, :].rearrange("p (m t) -> p t m", t=PACK)
+            )
+
+        deal_scales(0)
+        w4_dealt = tile([P, PACK, P, 2], U8, "w4_dealt")
+        nc.vector.tensor_copy(
+            out=w4_dealt[:], in_=w4_raw[:].rearrange("p (m t b) -> p t m b", t=PACK, b=2)
+        )
+
+        picked = [[tile([P, HALF], U32, "picked%d_%d" % (a, u)) for u in range(2)] for a in range(PASSES)]
+
+        def pick(a, u):
+            nc.vector.tensor_copy(picked[a][u][:], table[a][:].indirect(entries(idx, u * HALF, HALF)))
+
+        EARLY = 6
+        a_banks = {}
+
+        def first_product(c, a):
+            if a == 0:
+                a_banks[c] = bank([P, PACK, CHUNK], "a_bank%d" % c, c % EARLY)
+            u, first = divmod(c * CHUNK, HALF)
+            for t in range(PACK):
+                nc.tensor.matmul_mx(
+                    out=a_banks[c][:, t, :],
+                    lhsT=w1_codes[a][:, t * P : (t + 1) * P].bitcast(FP8X4),
+                    lhsT_scale=w1_scales[a][:, t * P : (t + 1) * P],
+                    rhs=picked[a][u][:, first : first + CHUNK].bitcast(FP8X4),
+                    rhs_scale=picked_scales[4 * a : P, c * CHUNK : (c + 1) * CHUNK],
+                    start=(a == 0 and t == 0),
+                    stop=(a == PASSES - 1 and t == PACK - 1),
+                )
+
+        for a in range(PASSES - 1):
+            for u in range(2):
+                pick(a, u)
+            for c in range(EARLY):
+                first_product(c, a)
+        for u in range(2):
+            pick(PASSES - 1, u)
+
+        a_full = tile([P, PACK, S], F32, "a_full", "square")
+        h = [tile([P, 2, S], F32, "h%d" % u, "wide%d" % u) for u in range(2)]
+
+        def features(r):
+            a_woven = tile([P, RUN, PACK], BF16, "a_woven%d" % r)
+            chunks = range(2 * r, 2 * r + 2)
+            for c in chunks:
+                for a in range(PASSES):
+                    if c >= EARLY or a == PASSES - 1:
+                        first_product(c, a)
+            for c in chunks:
+                nc.scalar.copy(
+                    out=a_woven[:, (c % 2) * CHUNK : (c % 2 + 1) * CHUNK, :],
+                    in_=a_banks[c][:].rearrange("p t j -> p j t"),
+                )
+            for c in chunks:
+                nc.scalar.copy(out=a_full[:, :, c * CHUNK : (c + 1) * CHUNK], in_=a_banks[c][:])
+            a_codes = tile([P, RUN], U32, "a_codes%d" % r)
+            a_scales = tile([P, RUN], U8, "a_scales%d" % r)
+            nc.vector.quantize_mx(
+                out=a_codes[:].bitcast(FP8X4), scales=a_scales[:],
+                in_=a_woven[:].rearrange("p j t -> p (j t)"),
+            )
+            for u in range(2):
+                b_bank = bank([P, 2, RUN], "b_bank%d_%d" % (r, u), EARLY + u)
+                for i in range(2):
+                    t = 2 * u + i
+                    nc.tensor.matmul_mx(
+                        out=b_bank[:, i, :],
+                        lhsT=w4_dealt[:, t, :, :].rearrange("p m b -> p (m b)").bitcast(FP4X4),
+                        lhsT_scale=dealt_scales[:, 0, t, :],
+                        rhs=a_codes[:].bitcast(FP8X4),
+                        rhs_scale=a_scales[:],
+                        start=True,
+                        stop=True,
+                    )
+                nc.vector.tensor_tensor(
+                    h[u][:, :, r * RUN : (r + 1) * RUN],
+                    b_bank[:],
+                    a_full[:, 2 * u : 2 * u + 2, r * RUN : (r + 1) * RUN],
+                    ALU.mult,
+                )
+
+        def put(t, first, count):
+            nc.vector.tensor_tensor(
+                page[t][:].indirect(entries(idx2, first, count)),
+                h[t // 2][:, t % 2, first : first + count],
+                gain[:, t, first : first + count],
+                ALU.mult,
+            )
+
+        features(0)
+        put(0, 0, RUN)
+        put(1, 0, RUN)
+        features(1)
+        put(0, RUN, RUN)
+        put(1, RUN, RUN)
+        features(2)
+        put(2, 0, HALF)
+        features(3)
+        put(3, 0, HALF)
+
+        deal_scales(1)
+        w8_dealt = tile([P, PACK, P], I32, "w8_dealt")
+        nc.vector.tensor_copy(out=w8_dealt[:], in_=w8_raw[:].rearrange("p (m t) -> p t m", t=PACK))
+
+        x_woven = [tile([P, HALF, PACK], BF16, "x_woven%d" % u, "narrow%d" % u) for u in range(2)]
+
+        def reread(t):
+            seen = tile([P, M], F32, "seen%d" % t)
+            nc.vector.tensor_copy(seen[:], page[t][:].indirect(idx3[:]))
+            nc.scalar.activation(out=seen[:], in_=seen[:], func=ACT.Tanh, scale=sc_rows[:, t : t + 1])
+            for u in range(2):
+                nc.scalar.activation(
+                    out=x_woven[u][:, :, t], in_=seen[:, u * HALF : (u + 1) * HALF],
+                    func=ACT.Copy, scale=amp_rows[:, t : t + 1],
+                )
+
+        def adjoin(target, t):
+            nc.vector.tensor_copy(target, page[t][:].indirect(idx4[:]))
+
+        put(0, HALF, HALF)
+        put(1, HALF, HALF)
+        reread(0)
+        put(2, HALF, HALF)
+        reread(1)
+        reread(2)
+        put(3, HALF, HALF)
+        first = tile([P, M], F32, "adjoining0", "wide0")
+        adjoin(first[:], 0)
+        reread(3)
+        middle = tile([P, 2, M], F32, "adjoining12", "wide1")
+        adjoining = [first[:], middle[:, 0, :], middle[:, 1, :]]
+        adjoin(adjoining[1], 1)
+        adjoin(adjoining[2], 2)
+
+        x_codes, x_scales = [], []
+        for u in range(2):
+            codes = tile([P, HALF], U32, "x_codes%d" % u)
+            scales = tile([P, HALF], U8, "x_scales%d" % u)
+            nc.vector.quantize_mx(
+                out=codes[:].bitcast(FP8X4), scales=scales[:],
+                in_=x_woven[u][:].rearrange("p m t -> p (m t)"),
+            )
+            x_codes.append(codes)
+            x_scales.append(scales)
+
+        last = tile([P, M], F32, "adjoining3", "narrow1")
+        adjoin(last[:], 3)
+        adjoining.append(last[:])
+
+        y_size = tile([P, PACK, M], F32, "y_size", "square")
+        out_rows = out.rearrange("(p t) m -> t p m", t=PACK)
+        for u in range(2):
+            for t in range(PACK):
+                y_bank = bank([P, HALF], "y_bank%d_%d" % (u, t), PACK * u + t)
+                nc.tensor.matmul_mx(
+                    out=y_bank[:],
+                    lhsT=w8_dealt[:, t, :].bitcast(FP8X4),
+                    lhsT_scale=dealt_scales[:, 1, t, :],
+                    rhs=x_codes[u][:].bitcast(FP8X4),
+                    rhs_scale=x_scales[u][:],
+                    start=True,
+                    stop=True,
+                )
+                nc.scalar.activation(
+                    out=y_size[:, t, u * HALF : (u + 1) * HALF], in_=y_bank[:], func=ACT.Abs
+                )
+        for u in range(2):
+            for t in range(PACK):
+                cols = slice(u * HALF, (u + 1) * HALF)
+                nc.vector.scalar_tensor_tensor(
+                    out=adjoining[t][:, cols], in0=adjoining[t][:, cols],
+                    scalar=beta_rows[:, t : t + 1], in1=y_size[:, t, cols],
+                    op0=ALU.mult, op1=ALU.subtract,
+                )
+                nc.sync.dma_start(out=out_rows[t][:, cols], in_=adjoining[t][:, cols])

@@ -58,9 +58,9 @@ def tile_list_marble_bench_register_kernel(
                 in_=tab_scales[:, 4 * q : 4 * q + 4, :].bitcast(I32),
             )
 
-        def load_weight_scales(i, source):
+        def load_weight_scales(i, source, queue):
             for q in range(4):
-                nc.sync.dma_start(
+                queue.dma_start(
                     out=weight_scales[32 * q : 32 * q + 4, i, :].bitcast(I32),
                     in_=source[0, 4 * q : 4 * q + 4, :].bitcast(I32),
                 )
@@ -96,32 +96,34 @@ def tile_list_marble_bench_register_kernel(
         sc_rows = load_factor(sc, "sc_rows")
         load_w1(1)
         load_w1(2)
-        load_weight_scales(0, w4_scales)
+        load_weight_scales(0, w4_scales, nc.sync)
         load_table(1)
         load_table(2)
         w8_raw = tile([P, H], I32, "w8_raw")
         nc.sync.dma_start(out=w8_raw[:], in_=w8_words[0].rearrange("p c i -> p (c i)").bitcast(I32))
-        load_weight_scales(1, w8_scales)
+        load_weight_scales(1, w8_scales, nc.gpsimd)
 
         page = [tile([P, T2], F32, "page%d" % t) for t in range(PACK)]
         gain = tile([P, PACK, S], F32, "gain")
         page_rows = page0.rearrange("(p t) c -> t p c", t=PACK)
         gain_rows = wgs.rearrange("(p t) j -> p t j", t=PACK)
 
-        def load_gain(first, count):
+        def load_gain(tiles, first, count):
             for q in (0, 2, 1, 3):
                 nc.sync.dma_start(
-                    out=gain[32 * q : 32 * q + 32, :, first : first + count],
-                    in_=gain_rows[:, :, first : first + count],
+                    out=gain[32 * q : 32 * q + 32, tiles, first : first + count],
+                    in_=gain_rows[:, tiles, first : first + count],
                 )
 
         nc.sync.dma_start(out=page[0][:], in_=page_rows[0])
-        load_gain(0, RUN)
+        load_gain(slice(0, 2), 0, RUN)
         nc.sync.dma_start(out=page[1][:], in_=page_rows[1])
-        load_gain(RUN, RUN)
+        load_gain(slice(0, 2), RUN, RUN)
         nc.sync.dma_start(out=page[2][:], in_=page_rows[2])
+        load_gain(slice(2, 3), 0, HALF)
+        load_gain(slice(0, 3), HALF, HALF)
         nc.sync.dma_start(out=page[3][:], in_=page_rows[3])
-        load_gain(HALF, HALF)
+        load_gain(slice(3, 4), 0, S)
         amp_rows = load_factor(amp, "amp_rows")
         beta_rows = load_factor(beta, "beta_rows")
 
@@ -144,14 +146,15 @@ def tile_list_marble_bench_register_kernel(
         picked_scales = tile([P, S], U8, "picked_scales")
         nc.vector.tensor_copy(picked_scales[:], table_scales[:].indirect(idx[:]))
 
-        dealt_scales = tile([P, 2, PACK, P], U8, "dealt_scales")
-
-        def deal_scales(i):
+        def deal_scales(i, name, tag):
+            dealt = tile([P, PACK, P], U8, name, tag)
             nc.vector.tensor_copy(
-                out=dealt_scales[:, i, :, :], in_=weight_scales[:, i, :].rearrange("p (m t) -> p t m", t=PACK)
+                out=dealt[:], in_=weight_scales[:, i, :].rearrange("p (m t) -> p t m", t=PACK)
             )
+            return dealt
 
-        deal_scales(0)
+        w4_scales_dealt = deal_scales(0, "w4_scales_dealt", None)
+        w8_scales_dealt = deal_scales(1, "w8_scales_dealt", None)
         w4_dealt = tile([P, PACK, P, 2], U8, "w4_dealt")
         nc.vector.tensor_copy(
             out=w4_dealt[:], in_=w4_raw[:].rearrange("p (m t b) -> p t m b", t=PACK, b=2)
@@ -189,103 +192,128 @@ def tile_list_marble_bench_register_kernel(
             pick(PASSES - 1, u)
 
         a_full = tile([P, PACK, S], F32, "a_full", "square")
-        h = [tile([P, 2, S], F32, "h%d" % u, "wide%d" % u) for u in range(2)]
+        a_codes = tile([P, S], U32, "a_codes")
+        a_scales = tile([P, S], U8, "a_scales")
 
-        def features(r):
-            a_woven = tile([P, RUN, PACK], BF16, "a_woven%d" % r)
-            chunks = range(2 * r, 2 * r + 2)
-            for c in chunks:
-                for a in range(PASSES):
-                    if c >= EARLY or a == PASSES - 1:
-                        first_product(c, a)
-            for c in chunks:
-                nc.scalar.copy(
-                    out=a_woven[:, (c % 2) * CHUNK : (c % 2 + 1) * CHUNK, :],
-                    in_=a_banks[c][:].rearrange("p t j -> p j t"),
-                )
-            for c in chunks:
-                nc.scalar.copy(out=a_full[:, :, c * CHUNK : (c + 1) * CHUNK], in_=a_banks[c][:])
-            a_codes = tile([P, RUN], U32, "a_codes%d" % r)
-            a_scales = tile([P, RUN], U8, "a_scales%d" % r)
+        def quantise_a(first, count, tag):
+            a_woven = tile([P, count, PACK], BF16, "a_woven%d" % first, tag)
+            chunks = range(first // CHUNK, (first + count) // CHUNK)
+            for pair in range(chunks.start, chunks.stop, 2):
+                for c in (pair, pair + 1):
+                    for a in range(PASSES):
+                        if c >= EARLY or a == PASSES - 1:
+                            first_product(c, a)
+                if pair >= EARLY:
+                    for c in (pair, pair + 1):
+                        nc.scalar.copy(out=a_full[:, :, c * CHUNK : (c + 1) * CHUNK], in_=a_banks[c][:])
+                for c in (pair, pair + 1):
+                    weave = nc.vector.tensor_copy if c == 1 else nc.scalar.copy
+                    weave(
+                        out=a_woven[:, c * CHUNK - first : (c + 1) * CHUNK - first, :],
+                        in_=a_banks[c][:].rearrange("p t j -> p j t"),
+                    )
+                if pair < EARLY:
+                    for c in (pair, pair + 1):
+                        nc.scalar.copy(out=a_full[:, :, c * CHUNK : (c + 1) * CHUNK], in_=a_banks[c][:])
             nc.vector.quantize_mx(
-                out=a_codes[:].bitcast(FP8X4), scales=a_scales[:],
+                out=a_codes[:, first : first + count].bitcast(FP8X4),
+                scales=a_scales[:, first : first + count],
                 in_=a_woven[:].rearrange("p j t -> p (j t)"),
             )
-            for u in range(2):
-                b_bank = bank([P, 2, RUN], "b_bank%d_%d" % (r, u), EARLY + u)
-                for i in range(2):
-                    t = 2 * u + i
-                    nc.tensor.matmul_mx(
-                        out=b_bank[:, i, :],
-                        lhsT=w4_dealt[:, t, :, :].rearrange("p m b -> p (m b)").bitcast(FP4X4),
-                        lhsT_scale=dealt_scales[:, 0, t, :],
-                        rhs=a_codes[:].bitcast(FP8X4),
-                        rhs_scale=a_scales[:],
-                        start=True,
-                        stop=True,
-                    )
-                nc.vector.tensor_tensor(
-                    h[u][:, :, r * RUN : (r + 1) * RUN],
-                    b_bank[:],
-                    a_full[:, 2 * u : 2 * u + 2, r * RUN : (r + 1) * RUN],
-                    ALU.mult,
-                )
+
+        def second_product(target, t, first, count):
+            nc.tensor.matmul_mx(
+                out=target,
+                lhsT=w4_dealt[:, t, :, :].rearrange("p m b -> p (m b)").bitcast(FP4X4),
+                lhsT_scale=w4_scales_dealt[:, t, :],
+                rhs=a_codes[:, first : first + count].bitcast(FP8X4),
+                rhs_scale=a_scales[:, first : first + count],
+                start=True,
+                stop=True,
+            )
+
+        h = {}
+
+        def make_h(target, b, t, first, count):
+            nc.vector.tensor_tensor(target, b, a_full[:, t, first : first + count], ALU.mult)
+            h[t, first] = target
 
         def put(t, first, count):
             nc.vector.tensor_tensor(
                 page[t][:].indirect(entries(idx2, first, count)),
-                h[t // 2][:, t % 2, first : first + count],
+                h[t, first],
                 gain[:, t, first : first + count],
                 ALU.mult,
             )
 
-        features(0)
-        put(0, 0, RUN)
-        put(1, 0, RUN)
-        features(1)
-        put(0, RUN, RUN)
-        put(1, RUN, RUN)
-        features(2)
-        put(2, 0, HALF)
-        features(3)
-        put(3, 0, HALF)
+        def wide_b(t, first, number):
+            b_bank = bank([P, HALF], "b_bank%d_%d" % (t, first), number)
+            second_product(b_bank[:], t, first, HALF)
+            return b_bank
 
-        deal_scales(1)
-        w8_dealt = tile([P, PACK, P], I32, "w8_dealt")
-        nc.vector.tensor_copy(out=w8_dealt[:], in_=w8_raw[:].rearrange("p (m t) -> p t m", t=PACK))
+
+        h01 = tile([P, 2, S], F32, "h01", "wide0")
+        for r in range(2):
+            first = r * RUN
+            quantise_a(first, RUN, "a_woven_run%d" % r)
+            if r == 0:
+                w8_dealt = tile([P, PACK, P], I32, "w8_dealt", "a_woven_run0")
+                nc.vector.tensor_copy(out=w8_dealt[:], in_=w8_raw[:].rearrange("p (m t) -> p t m", t=PACK))
+            for t in range(2):
+                b_bank = bank([P, RUN], "b_bank_run%d_%d" % (r, t), EARLY + t)
+                second_product(b_bank[:], t, first, RUN)
+                make_h(h01[:, t, first : first + RUN], b_bank[:], t, first, RUN)
+            for t in range(2):
+                put(t, first, RUN)
+
+        quantise_a(HALF, HALF, "a_woven_half")
+        b_early = [wide_b(t, 0, t - 2) for t in range(2, PACK)]
+        b_late = [wide_b(t, HALF, (EARLY + t) if t < 2 else t) for t in range(PACK)]
+        h23_early = tile([P, 2, HALF], F32, "h23_early")
+        h23_late = tile([P, 2, HALF], F32, "h23_late", "wide1")
+        for t in range(2, PACK):
+            make_h(h23_early[:, t - 2, :], b_early[t - 2][:], t, 0, HALF)
+        put(2, 0, HALF)
+        for t in range(2):
+            make_h(h01[:, t, HALF:S], b_late[t][:], t, HALF, HALF)
 
         x_woven = [tile([P, HALF, PACK], BF16, "x_woven%d" % u, "narrow%d" % u) for u in range(2)]
 
-        def reread(t):
+        def reread(t, pieces):
+            width = M // pieces
             seen = tile([P, M], F32, "seen%d" % t)
-            nc.vector.tensor_copy(seen[:], page[t][:].indirect(idx3[:]))
-            nc.scalar.activation(out=seen[:], in_=seen[:], func=ACT.Tanh, scale=sc_rows[:, t : t + 1])
+            for first in range(0, M, width):
+                nc.vector.tensor_copy(
+                    seen[:, first : first + width], page[t][:].indirect(entries(idx3, first, width))
+                )
             for u in range(2):
+                bounded = tile([P, HALF], F32, "bounded%d_%d" % (t, u), "bounded%d" % u)
                 nc.scalar.activation(
-                    out=x_woven[u][:, :, t], in_=seen[:, u * HALF : (u + 1) * HALF],
-                    func=ACT.Copy, scale=amp_rows[:, t : t + 1],
+                    out=bounded[:], in_=seen[:, u * HALF : (u + 1) * HALF],
+                    func=ACT.Tanh, scale=sc_rows[:, t : t + 1],
+                )
+                nc.scalar.activation(
+                    out=x_woven[u][:, :, t], in_=bounded[:], func=ACT.Copy, scale=amp_rows[:, t : t + 1]
                 )
 
         def adjoin(target, t):
             nc.vector.tensor_copy(target, page[t][:].indirect(idx4[:]))
 
         put(0, HALF, HALF)
+        for t in range(2, PACK):
+            make_h(h23_late[:, t - 2, :], b_late[t][:], t, HALF, HALF)
         put(1, HALF, HALF)
-        reread(0)
+        reread(0, 1)
         put(2, HALF, HALF)
-        reread(1)
-        reread(2)
+        reread(1, 1)
+        put(3, 0, HALF)
+        reread(2, 1)
         put(3, HALF, HALF)
-        first = tile([P, M], F32, "adjoining0", "wide0")
-        adjoin(first[:], 0)
-        reread(3)
-        middle = tile([P, 2, M], F32, "adjoining12", "wide1")
-        adjoining = [first[:], middle[:, 0, :], middle[:, 1, :]]
-        adjoin(adjoining[1], 1)
-        adjoin(adjoining[2], 2)
+        reread(3, 2)
 
         x_codes, x_scales = [], []
-        for u in range(2):
+
+        def quantise_x(u):
             codes = tile([P, HALF], U32, "x_codes%d" % u)
             scales = tile([P, HALF], U8, "x_scales%d" % u)
             nc.vector.quantize_mx(
@@ -295,9 +323,16 @@ def tile_list_marble_bench_register_kernel(
             x_codes.append(codes)
             x_scales.append(scales)
 
-        last = tile([P, M], F32, "adjoining3", "narrow1")
-        adjoin(last[:], 3)
-        adjoining.append(last[:])
+        first = tile([P, M], F32, "adjoining0", "wide1")
+        adjoin(first[:], 0)
+        quantise_x(0)
+        second = tile([P, M], F32, "adjoining1", "bounded0")
+        adjoin(second[:], 1)
+        quantise_x(1)
+        last = tile([P, 2, M], F32, "adjoining23", "bounded1")
+        adjoining = [first[:], second[:], last[:, 0, :], last[:, 1, :]]
+        adjoin(adjoining[2], 2)
+        adjoin(adjoining[3], 3)
 
         y_size = tile([P, PACK, M], F32, "y_size", "square")
         out_rows = out.rearrange("(p t) m -> t p m", t=PACK)
@@ -307,7 +342,7 @@ def tile_list_marble_bench_register_kernel(
                 nc.tensor.matmul_mx(
                     out=y_bank[:],
                     lhsT=w8_dealt[:, t, :].bitcast(FP8X4),
-                    lhsT_scale=dealt_scales[:, 1, t, :],
+                    lhsT_scale=w8_scales_dealt[:, t, :],
                     rhs=x_codes[u][:].bitcast(FP8X4),
                     rhs_scale=x_scales[u][:],
                     start=True,
@@ -316,12 +351,30 @@ def tile_list_marble_bench_register_kernel(
                 nc.scalar.activation(
                     out=y_size[:, t, u * HALF : (u + 1) * HALF], in_=y_bank[:], func=ACT.Abs
                 )
-        for u in range(2):
-            for t in range(PACK):
-                cols = slice(u * HALF, (u + 1) * HALF)
+
+        def finish(t, u):
+            cols = slice(u * HALF, (u + 1) * HALF)
+            if t < 2:
+                nc.gpsimd.tensor_tensor(adjoining[t][:, cols], adjoining[t][:, cols], y_size[:, t, cols], ALU.subtract)
+            else:
                 nc.vector.scalar_tensor_tensor(
                     out=adjoining[t][:, cols], in0=adjoining[t][:, cols],
                     scalar=beta_rows[:, t : t + 1], in1=y_size[:, t, cols],
                     op0=ALU.mult, op1=ALU.subtract,
                 )
-                nc.sync.dma_start(out=out_rows[t][:, cols], in_=adjoining[t][:, cols])
+            nc.sync.dma_start(out=out_rows[t][:, cols], in_=adjoining[t][:, cols])
+
+        def scale_adjoining(t):
+            nc.gpsimd.tensor_scalar(
+                adjoining[t], adjoining[t], beta_rows[:, t : t + 1], 0.0, ALU.mult, ALU.add
+            )
+
+        scale_adjoining(0)
+        finish(0, 0)
+        scale_adjoining(1)
+        finish(1, 0)
+        finish(0, 1)
+        finish(1, 1)
+        for u in range(2):
+            for t in range(2, PACK):
+                finish(t, u)

@@ -98,10 +98,10 @@ def tile_list_marble_bench_register_kernel(
         load_w1(2)
         load_weight_scales(0, w4_scales, nc.sync)
         load_table(1)
+        load_weight_scales(1, w8_scales, nc.sync)
         load_table(2)
         w8_raw = tile([P, H], I32, "w8_raw")
         nc.sync.dma_start(out=w8_raw[:], in_=w8_words[0].rearrange("p c i -> p (c i)").bitcast(I32))
-        load_weight_scales(1, w8_scales, nc.gpsimd)
 
         page = [tile([P, T2], F32, "page%d" % t) for t in range(PACK)]
         gain = tile([P, PACK, S], F32, "gain")
@@ -130,7 +130,8 @@ def tile_list_marble_bench_register_kernel(
         w1_codes, w1_scales = [], []
         for a in range(PASSES):
             woven = tile([P, PACK, P, PACK], BF16, "w1_woven%d" % a, "narrow%d" % a)
-            nc.scalar.copy(
+            cast = nc.vector.tensor_copy if a == 1 else nc.scalar.copy
+            cast(
                 out=woven[:].rearrange("p t m j -> p m j t"),
                 in_=w1_raw[a][:].rearrange("p j (m t) -> p m j t", t=PACK),
             )
@@ -154,7 +155,6 @@ def tile_list_marble_bench_register_kernel(
             return dealt
 
         w4_scales_dealt = deal_scales(0, "w4_scales_dealt", None)
-        w8_scales_dealt = deal_scales(1, "w8_scales_dealt", None)
         w4_dealt = tile([P, PACK, P, 2], U8, "w4_dealt")
         nc.vector.tensor_copy(
             out=w4_dealt[:], in_=w4_raw[:].rearrange("p (m t b) -> p t m b", t=PACK, b=2)
@@ -170,7 +170,7 @@ def tile_list_marble_bench_register_kernel(
 
         def first_product(c, a):
             if a == 0:
-                a_banks[c] = bank([P, PACK, CHUNK], "a_bank%d" % c, c % EARLY)
+                a_banks[c] = bank([P, PACK, CHUNK], "a_bank%d" % c, c)
             u, first = divmod(c * CHUNK, HALF)
             for t in range(PACK):
                 nc.tensor.matmul_mx(
@@ -188,6 +188,7 @@ def tile_list_marble_bench_register_kernel(
                 pick(a, u)
             for c in range(EARLY):
                 first_product(c, a)
+        w8_scales_dealt = deal_scales(1, "w8_scales_dealt", None)
         for u in range(2):
             pick(PASSES - 1, u)
 
@@ -260,15 +261,15 @@ def tile_list_marble_bench_register_kernel(
                 w8_dealt = tile([P, PACK, P], I32, "w8_dealt", "a_woven_run0")
                 nc.vector.tensor_copy(out=w8_dealt[:], in_=w8_raw[:].rearrange("p (m t) -> p t m", t=PACK))
             for t in range(2):
-                b_bank = bank([P, RUN], "b_bank_run%d_%d" % (r, t), EARLY + t)
+                b_bank = bank([P, RUN], "b_bank_run%d_%d" % (r, t), t + (EARLY if r == 0 else 0))
                 second_product(b_bank[:], t, first, RUN)
                 make_h(h01[:, t, first : first + RUN], b_bank[:], t, first, RUN)
             for t in range(2):
                 put(t, first, RUN)
 
         quantise_a(HALF, HALF, "a_woven_half")
-        b_early = [wide_b(t, 0, t - 2) for t in range(2, PACK)]
-        b_late = [wide_b(t, HALF, (EARLY + t) if t < 2 else t) for t in range(PACK)]
+        b_early = [wide_b(t, 0, EARLY + t - 2) for t in range(2, PACK)]
+        b_late = [wide_b(t, HALF, t) for t in range(PACK)]
         h23_early = tile([P, 2, HALF], F32, "h23_early")
         h23_late = tile([P, 2, HALF], F32, "h23_late", "wide1")
         for t in range(2, PACK):
@@ -329,12 +330,15 @@ def tile_list_marble_bench_register_kernel(
         second = tile([P, M], F32, "adjoining1", "bounded0")
         adjoin(second[:], 1)
         quantise_x(1)
-        last = tile([P, 2, M], F32, "adjoining23", "bounded1")
-        adjoining = [first[:], second[:], last[:, 0, :], last[:, 1, :]]
-        adjoin(adjoining[2], 2)
-        adjoin(adjoining[3], 3)
+        third = tile([P, M], F32, "adjoining2", "bounded1")
+        adjoin(third[:], 2)
+        adjoining = {}
+        for t, whole in enumerate((first, second, third)):
+            for u in range(2):
+                adjoining[t, u] = whole[:, u * HALF : (u + 1) * HALF]
 
-        y_size = tile([P, PACK, M], F32, "y_size", "square")
+        y_rest = tile([P, PACK - 1, M], F32, "y_rest", "square")
+        y_size = {}
         out_rows = out.rearrange("(p t) m -> t p m", t=PACK)
         for u in range(2):
             for t in range(PACK):
@@ -348,33 +352,27 @@ def tile_list_marble_bench_register_kernel(
                     start=True,
                     stop=True,
                 )
-                nc.scalar.activation(
-                    out=y_size[:, t, u * HALF : (u + 1) * HALF], in_=y_bank[:], func=ACT.Abs
-                )
+                if t == 0:
+                    y_size[t, u] = tile([P, HALF], F32, "y_first%d" % u, "seen%d" % u)[:]
+                else:
+                    y_size[t, u] = y_rest[:, t - 1, u * HALF : (u + 1) * HALF]
+                nc.scalar.activation(out=y_size[t, u], in_=y_bank[:], func=ACT.Abs)
 
         def finish(t, u):
-            cols = slice(u * HALF, (u + 1) * HALF)
-            if t < 2:
-                nc.gpsimd.tensor_tensor(adjoining[t][:, cols], adjoining[t][:, cols], y_size[:, t, cols], ALU.subtract)
-            else:
-                nc.vector.scalar_tensor_tensor(
-                    out=adjoining[t][:, cols], in0=adjoining[t][:, cols],
-                    scalar=beta_rows[:, t : t + 1], in1=y_size[:, t, cols],
-                    op0=ALU.mult, op1=ALU.subtract,
-                )
-            nc.sync.dma_start(out=out_rows[t][:, cols], in_=adjoining[t][:, cols])
-
-        def scale_adjoining(t):
-            nc.gpsimd.tensor_scalar(
-                adjoining[t], adjoining[t], beta_rows[:, t : t + 1], 0.0, ALU.mult, ALU.add
+            nc.vector.scalar_tensor_tensor(
+                out=adjoining[t, u], in0=adjoining[t, u],
+                scalar=beta_rows[:, t : t + 1], in1=y_size[t, u],
+                op0=ALU.mult, op1=ALU.subtract,
             )
+            nc.sync.dma_start(out=out_rows[t][:, u * HALF : (u + 1) * HALF], in_=adjoining[t, u])
 
-        scale_adjoining(0)
-        finish(0, 0)
-        scale_adjoining(1)
-        finish(1, 0)
-        finish(0, 1)
-        finish(1, 1)
+        def adjoin_last(u):
+            adjoining[3, u] = tile([P, HALF], F32, "adjoining3_%d" % u, "seen%d" % u)[:]
+            nc.vector.tensor_copy(adjoining[3, u], page[3][:].indirect(entries(idx4, u * HALF, HALF)))
+
         for u in range(2):
-            for t in range(2, PACK):
-                finish(t, u)
+            finish(0, u)
+            finish(1, u)
+            adjoin_last(u)
+            finish(2, u)
+            finish(3, u)

from contextlib import ExitStack

import concourse.mybir as mybir

K, H, T, S, T2, M = 1536, 512, 4096, 1024, 2048, 1024
FLOPS = 2 * K * H * S + 2 * H * H * S + 2 * H * H * M

F32 = mybir.dt.float32
BF16 = mybir.dt.bfloat16
I32 = mybir.dt.int32
U32 = mybir.dt.uint32
U16 = mybir.dt.uint16
U8 = mybir.dt.uint8
FP8X4 = mybir.dt.float8_e4m3fn_x4
FP4X4 = mybir.dt.float4_e2m1fn_x4
ALU = mybir.AluOpType
ACT = mybir.ActivationFunctionType

P = 128
PACK = 4
PASSES = K // (P * PACK)
CHUNK = 128
HALF = 512
RUN = 256


def tile_list_marble_bench_register_kernel(
    tc, tab_words, tab_scales, offs, offs2, offs3, offs4, w1, w4_words, w4_scales,
    w8_words, w8_scales, wgs, page0, sc, amp, beta, out,
):
    nc = tc.nc
    with ExitStack() as ctx:
        lists = ctx.enter_context(tc.tile_pool(name="lists", bufs=1))
        keep = ctx.enter_context(tc.tile_pool(name="keep", bufs=1))
        psum = ctx.enter_context(tc.psum_pool(name="psum", bufs=1))

        def tile(shape, dtype, name, tag=None):
            return keep.tile(shape, dtype, name=name, tag=tag or name, align_bytes=64)

        def bank(shape, name, number):
            return psum.tile(shape, F32, name=name, tag="bank%d" % number)

        def load_list(source, name):
            held = lists.tile([P, S // 16], U16, name=name)
            nc.sync.dma_start(held[:], source)
            return held

        def entries(held, first, count):
            return held[:, first // 16 : (first + count) // 16]

        table_scales = tile([P, T], U8, "table_scales")
        nc.vector.memset(table_scales[:].bitcast(I32), 0)
        weight_scales = tile([P, 2, H], U8, "weight_scales")
        nc.vector.memset(weight_scales[:].rearrange("p i c -> p (i c)").bitcast(I32), 0)
        for q in range(4):
            nc.gpsimd.dma_start(
                out=table_scales[32 * q : 32 * q + 4 * PASSES, :].bitcast(I32),
                in_=tab_scales[:, 4 * q : 4 * q + 4, :].bitcast(I32),
            )

        def load_weight_scales(i, source, queue):
            for q in range(4):
                queue.dma_start(
                    out=weight_scales[32 * q : 32 * q + 4, i, :].bitcast(I32),
                    in_=source[0, 4 * q : 4 * q + 4, :].bitcast(I32),
                )

        def load_factor(source, name):
            factor = tile([P, PACK], F32, name)
            nc.sync.dma_start(out=factor[:], in_=source.rearrange("(p t) -> p t", t=PACK))
            return factor

        table = [tile([P, T], U32, "table%d" % a) for a in range(PASSES)]
        w1_raw = [tile([P, PACK, H], F32, "w1_raw%d" % a, "wide%d" % a) for a in range(PASSES)]

        def load_table(a):
            nc.sync.dma_start(
                out=table[a][:].bitcast(I32),
                in_=tab_words[a].rearrange("p t i -> p (t i)").bitcast(I32),
            )

        def load_w1(a):
            nc.sync.dma_start(
                out=w1_raw[a][:],
                in_=w1[a * HALF : (a + 1) * HALF, :].rearrange("(p j) c -> p j c", j=PACK),
            )

        load_table(0)
        idx = load_list(offs, "idx")
        load_w1(0)
        w4_raw = tile([P, 2 * H], U8, "w4_raw")
        nc.sync.dma_start(out=w4_raw[:].bitcast(I32), in_=w4_words[0].bitcast(I32))
        idx2 = load_list(offs2, "idx2")
        idx3 = load_list(offs3, "idx3")
        idx4 = load_list(offs4, "idx4")
        sc_rows = load_factor(sc, "sc_rows")
        load_w1(1)
        load_w1(2)
        load_weight_scales(0, w4_scales, nc.sync)
        load_table(1)
        load_weight_scales(1, w8_scales, nc.sync)
        load_table(2)
        w8_raw = tile([P, H], I32, "w8_raw")
        nc.sync.dma_start(out=w8_raw[:], in_=w8_words[0].rearrange("p c i -> p (c i)").bitcast(I32))

        page = [tile([P, T2], F32, "page%d" % t) for t in range(PACK)]
        gain = tile([P, PACK, S], F32, "gain")
        page_rows = page0.rearrange("(p t) c -> t p c", t=PACK)
        gain_rows = wgs.rearrange("(p t) j -> p t j", t=PACK)

        def load_gain(tiles, first, count):
            for q in (0, 2, 1, 3):
                nc.sync.dma_start(
                    out=gain[32 * q : 32 * q + 32, tiles, first : first + count],
                    in_=gain_rows[:, tiles, first : first + count],
                )

        nc.sync.dma_start(out=page[0][:], in_=page_rows[0])
        load_gain(slice(0, 2), 0, RUN)
        nc.sync.dma_start(out=page[1][:], in_=page_rows[1])
        load_gain(slice(0, 2), RUN, RUN)
        nc.sync.dma_start(out=page[2][:], in_=page_rows[2])
        load_gain(slice(2, 3), 0, HALF)
        load_gain(slice(0, 3), HALF, HALF)
        nc.sync.dma_start(out=page[3][:], in_=page_rows[3])
        load_gain(slice(3, 4), 0, S)
        amp_rows = load_factor(amp, "amp_rows")
        beta_rows = load_factor(beta, "beta_rows")

        w1_codes, w1_scales = [], []
        for a in range(PASSES):
            woven = tile([P, PACK, P, PACK], BF16, "w1_woven%d" % a, "narrow%d" % a)
            cast = nc.vector.tensor_copy if a == 1 else nc.scalar.copy
            cast(
                out=woven[:].rearrange("p t m j -> p m j t"),
                in_=w1_raw[a][:].rearrange("p j (m t) -> p m j t", t=PACK),
            )
            codes = tile([P, H], U32, "w1_codes%d" % a)
            scales = tile([P, H], U8, "w1_scales%d" % a)
            nc.vector.quantize_mx(
                out=codes[:].bitcast(FP8X4), scales=scales[:],
                in_=woven[:].rearrange("p t m j -> p (t m j)"),
            )
            w1_codes.append(codes)
            w1_scales.append(scales)

        picked_scales = tile([P, S], U8, "picked_scales")
        nc.vector.tensor_copy(picked_scales[:], table_scales[:].indirect(idx[:]))

        def deal_scales(i, name, tag):
            dealt = tile([P, PACK, P], U8, name, tag)
            nc.vector.tensor_copy(
                out=dealt[:], in_=weight_scales[:, i, :].rearrange("p (m t) -> p t m", t=PACK)
            )
            return dealt

        w4_scales_dealt = deal_scales(0, "w4_scales_dealt", None)
        w4_dealt = tile([P, PACK, P, 2], U8, "w4_dealt")
        nc.vector.tensor_copy(
            out=w4_dealt[:], in_=w4_raw[:].rearrange("p (m t b) -> p t m b", t=PACK, b=2)
        )

        picked = [[tile([P, HALF], U32, "picked%d_%d" % (a, u)) for u in range(2)] for a in range(PASSES)]

        def pick(a, u):
            nc.vector.tensor_copy(picked[a][u][:], table[a][:].indirect(entries(idx, u * HALF, HALF)))

        EARLY = 6
        a_banks = {}

        def first_product(c, a):
            if a == 0:
                a_banks[c] = bank([P, PACK, CHUNK], "a_bank%d" % c, c)
            u, first = divmod(c * CHUNK, HALF)
            for t in range(PACK):
                nc.tensor.matmul_mx(
                    out=a_banks[c][:, t, :],
                    lhsT=w1_codes[a][:, t * P : (t + 1) * P].bitcast(FP8X4),
                    lhsT_scale=w1_scales[a][:, t * P : (t + 1) * P],
                    rhs=picked[a][u][:, first : first + CHUNK].bitcast(FP8X4),
                    rhs_scale=picked_scales[4 * a : P, c * CHUNK : (c + 1) * CHUNK],
                    start=(a == 0 and t == 0),
                    stop=(a == PASSES - 1 and t == PACK - 1),
                )

        for a in range(PASSES - 1):
            for u in range(2):
                pick(a, u)
            for c in range(EARLY):
                first_product(c, a)
        w8_scales_dealt = deal_scales(1, "w8_scales_dealt", None)
        for u in range(2):
            pick(PASSES - 1, u)

        a_full = tile([P, PACK, S], F32, "a_full", "square")
        a_codes = tile([P, S], U32, "a_codes")
        a_scales = tile([P, S], U8, "a_scales")

        def quantise_a(first, count, tag):
            a_woven = tile([P, count, PACK], BF16, "a_woven%d" % first, tag)
            chunks = range(first // CHUNK, (first + count) // CHUNK)
            for pair in range(chunks.start, chunks.stop, 2):
                for c in (pair, pair + 1):
                    for a in range(PASSES):
                        if c >= EARLY or a == PASSES - 1:
                            first_product(c, a)
                if pair >= EARLY:
                    for c in (pair, pair + 1):
                        nc.scalar.copy(out=a_full[:, :, c * CHUNK : (c + 1) * CHUNK], in_=a_banks[c][:])
                for c in (pair, pair + 1):
                    weave = nc.vector.tensor_copy if c == 1 else nc.scalar.copy
                    weave(
                        out=a_woven[:, c * CHUNK - first : (c + 1) * CHUNK - first, :],
                        in_=a_banks[c][:].rearrange("p t j -> p j t"),
                    )
                if pair < EARLY:
                    for c in (pair, pair + 1):
                        nc.scalar.copy(out=a_full[:, :, c * CHUNK : (c + 1) * CHUNK], in_=a_banks[c][:])
            nc.vector.quantize_mx(
                out=a_codes[:, first : first + count].bitcast(FP8X4),
                scales=a_scales[:, first : first + count],
                in_=a_woven[:].rearrange("p j t -> p (j t)"),
            )

        def second_product(target, t, first, count):
            nc.tensor.matmul_mx(
                out=target,
                lhsT=w4_dealt[:, t, :, :].rearrange("p m b -> p (m b)").bitcast(FP4X4),
                lhsT_scale=w4_scales_dealt[:, t, :],
                rhs=a_codes[:, first : first + count].bitcast(FP8X4),
                rhs_scale=a_scales[:, first : first + count],
                start=True,
                stop=True,
            )

        h = {}

        def make_h(target, b, t, first, count):
            nc.vector.tensor_tensor(target, b, a_full[:, t, first : first + count], ALU.mult)
            h[t, first] = target

        def put(t, first, count):
            nc.vector.tensor_tensor(
                page[t][:].indirect(entries(idx2, first, count)),
                h[t, first],
                gain[:, t, first : first + count],
                ALU.mult,
            )

        def wide_b(t, first, number):
            b_bank = bank([P, HALF], "b_bank%d_%d" % (t, first), number)
            second_product(b_bank[:], t, first, HALF)
            return b_bank


        h01 = tile([P, 2, S], F32, "h01", "wide0")
        for r in range(2):
            first = r * RUN
            quantise_a(first, RUN, "a_woven_run%d" % r)
            if r == 0:
                w8_dealt = tile([P, PACK, P], I32, "w8_dealt", "a_woven_run0")
                nc.vector.tensor_copy(out=w8_dealt[:], in_=w8_raw[:].rearrange("p (m t) -> p t m", t=PACK))
            for t in range(2):
                b_bank = bank([P, RUN], "b_bank_run%d_%d" % (r, t), t + (EARLY if r == 0 else 0))
                second_product(b_bank[:], t, first, RUN)
                make_h(h01[:, t, first : first + RUN], b_bank[:], t, first, RUN)
            for t in range(2):
                put(t, first, RUN)

        quantise_a(HALF, HALF, "a_woven_half")
        b_early = [wide_b(t, 0, EARLY + t - 2) for t in range(2, PACK)]
        b_late = [wide_b(t, HALF, t) for t in range(PACK)]
        h23_early = tile([P, 2, HALF], F32, "h23_early")
        h23_late = tile([P, 2, HALF], F32, "h23_late", "wide1")
        for t in range(2, PACK):
            make_h(h23_early[:, t - 2, :], b_early[t - 2][:], t, 0, HALF)
        put(2, 0, HALF)
        for t in range(2):
            make_h(h01[:, t, HALF:S], b_late[t][:], t, HALF, HALF)

        x_woven = [tile([P, HALF, PACK], BF16, "x_woven%d" % u, "narrow%d" % u) for u in range(2)]

        def reread(t, pieces):
            width = M // pieces
            seen = tile([P, M], F32, "seen%d" % t)
            for first in range(0, M, width):
                nc.vector.tensor_copy(
                    seen[:, first : first + width], page[t][:].indirect(entries(idx3, first, width))
                )
            for u in range(2):
                bounded = tile([P, HALF], F32, "bounded%d_%d" % (t, u), "bounded%d" % u)
                nc.scalar.activation(
                    out=bounded[:], in_=seen[:, u * HALF : (u + 1) * HALF],
                    func=ACT.Tanh, scale=sc_rows[:, t : t + 1],
                )
                nc.scalar.activation(
                    out=x_woven[u][:, :, t], in_=bounded[:], func=ACT.Copy, scale=amp_rows[:, t : t + 1]
                )

        def adjoin(target, t):
            nc.vector.tensor_copy(target, page[t][:].indirect(idx4[:]))

        put(0, HALF, HALF)
        for t in range(2, PACK):
            make_h(h23_late[:, t - 2, :], b_late[t][:], t, HALF, HALF)
        put(1, HALF, HALF)
        reread(0, 1)
        put(2, HALF, HALF)
        reread(1, 1)
        put(3, 0, HALF)
        reread(2, 1)
        put(3, HALF, HALF)
        reread(3, 2)

        x_codes, x_scales = [], []

        def quantise_x(u):
            codes = tile([P, HALF], U32, "x_codes%d" % u)
            scales = tile([P, HALF], U8, "x_scales%d" % u)
            nc.vector.quantize_mx(
                out=codes[:].bitcast(FP8X4), scales=scales[:],
                in_=x_woven[u][:].rearrange("p m t -> p (m t)"),
            )
            x_codes.append(codes)
            x_scales.append(scales)

        first = tile([P, M], F32, "adjoining0", "wide1")
        adjoin(first[:], 0)
        quantise_x(0)
        second = tile([P, M], F32, "adjoining1", "bounded0")
        adjoin(second[:], 1)
        quantise_x(1)
        third = tile([P, M], F32, "adjoining2", "bounded1")
        adjoin(third[:], 2)
        adjoining = {}
        for t, whole in enumerate((first, second, third)):
            for u in range(2):
                adjoining[t, u] = whole[:, u * HALF : (u + 1) * HALF]

        y_rest = tile([P, PACK - 1, M], F32, "y_rest", "square")
        y_size = {}
        out_rows = out.rearrange("(p t) m -> t p m", t=PACK)
        for u in range(2):
            for t in range(PACK):
                y_bank = bank([P, HALF], "y_bank%d_%d" % (u, t), PACK * u + t)
                nc.tensor.matmul_mx(
                    out=y_bank[:],
                    lhsT=w8_dealt[:, t, :].bitcast(FP8X4),
                    lhsT_scale=w8_scales_dealt[:, t, :],
                    rhs=x_codes[u][:].bitcast(FP8X4),
                    rhs_scale=x_scales[u][:],
                    start=True,
                    stop=True,
                )
                if t == 0:
                    y_size[t, u] = tile([P, HALF], F32, "y_first%d" % u, "seen%d" % u)[:]
                else:
                    y_size[t, u] = y_rest[:, t - 1, u * HALF : (u + 1) * HALF]
                nc.scalar.activation(out=y_size[t, u], in_=y_bank[:], func=ACT.Abs)

        def finish(t, u):
            nc.vector.scalar_tensor_tensor(
                out=adjoining[t, u], in0=adjoining[t, u],
                scalar=beta_rows[:, t : t + 1], in1=y_size[t, u],
                op0=ALU.mult, op1=ALU.subtract,
            )
            nc.sync.dma_start(out=out_rows[t][:, u * HALF : (u + 1) * HALF], in_=adjoining[t, u])

        def adjoin_last(u):
            adjoining[3, u] = tile([P, HALF], F32, "adjoining3_%d" % u, "seen%d" % u)[:]
            nc.vector.tensor_copy(adjoining[3, u], page[3][:].indirect(entries(idx4, u * HALF, HALF)))

        for u in range(2):
            finish(0, u)
            finish(1, u)
            adjoin_last(u)
            finish(2, u)
            finish(3, u)
